import numpy as np
import ml_dtypes

BF16 = ml_dtypes.bfloat16


def bf(x):
    return np.asarray(x, np.float32).astype(BF16)


def f32(x):
    return np.asarray(x, np.float32)


def f64(x):
    return np.asarray(x).astype(np.float64)


def striped(idx):
    return np.tile(idx.reshape(-1, 16).T, (8, 1))


def rows(idx, k):
    return np.tile(idx, (k, 1))


def look(tab, idx):
    return np.take_along_axis(f64(tab), rows(idx, len(tab)), axis=1)


K, S, V, N, M = 512, 2048, 1024, 1024, 256


def setup_inputs():
    return {"tab": bf(np.random.standard_normal((2, K, S))), "x0": bf(np.random.standard_normal((K, V))), "w": bf(np.random.standard_normal((K, M)) / np.sqrt(K)), "offs": striped(np.random.randint(0, S, N))}


def reference(tab, x0, w, offs):
    idx = offs[:16].T.reshape(-1)
    x = f64(x0) * look(tab[0], idx) + look(tab[1], idx)
    y = f64(w).T @ x
    return y

@@ -1,0 +1,78 @@
+import concourse.mybir as mybir
+
+F32, BF16, U16 = mybir.dt.float32, mybir.dt.bfloat16, mybir.dt.uint16
+MULT, ADD = mybir.AluOpType.mult, mybir.AluOpType.add
+
+P = 128
+PIECE = 512
+
+FLOPS = 2 * 512 * 1024 + 2 * 512 * 1024 * 256
+
+
+def tile_lookup_film_mul_none_kernel(tc, tab, x0, w, offs, out):
+    nc = tc.nc
+    rows, n = x0.shape
+    ids = tab.shape[2]
+    m = w.shape[1]
+    blocks, pieces, m_blocks = rows // P, n // PIECE, m // P
+
+    with (
+        tc.tile_pool(name="held", bufs=1) as held,
+        tc.psum_pool(name="psum", bufs=1) as psum,
+    ):
+        offsets = held.tile([P, n // 16], U16, name="offsets")
+        nc.sync.dma_start(offsets[:], offs)
+
+        x0_in, gains_in, shifts_in = [], [], []
+        for b in range(blocks):
+            r = slice(b * P, (b + 1) * P)
+            x0_in.append(held.tile([P, n], BF16, name=f"x0_in{b}"))
+            gains_in.append(held.tile([P, ids], BF16, name=f"gains_in{b}"))
+            shifts_in.append(held.tile([P, ids], BF16, name=f"shifts_in{b}"))
+            nc.sync.dma_start(x0_in[b][:], x0[r, :])
+            nc.sync.dma_start(gains_in[b][:], tab[0, r, :])
+            nc.sync.dma_start(shifts_in[b][:], tab[1, r, :])
+            if b == 0:
+                w_sb = held.tile([P, blocks, m], BF16, name="w_sb")
+                nc.sync.dma_start(w_sb[:], w.rearrange("(b p) m -> p b m", p=P))
+
+        banks = {}
+        for j in range(pieces):
+            for k in range(m_blocks):
+                banks[j, k] = psum.tile([P, PIECE], F32, name=f"bank{j}_{k}")
+
+        for b in range(blocks):
+            x0_f = held.tile([P, n], F32, name=f"x0_f{b}")
+            gains = held.tile([P, ids], F32, name=f"gains{b}")
+            shifts = held.tile([P, ids], F32, name=f"shifts{b}")
+            nc.vector.tensor_copy(x0_f[:], x0_in[b][:])
+            nc.scalar.copy(gains[:], gains_in[b][:])
+            nc.scalar.copy(shifts[:], shifts_in[b][:])
+
+            product = held.tile([P, n], F32, name=f"product{b}")
+            x_f = held.tile([P, n], F32, name=f"x_f{b}")
+            x_b = held.tile([P, n], BF16, name=f"x_b{b}")
+            lists = [offsets[:, j * (PIECE // 16) : (j + 1) * (PIECE // 16)] for j in range(pieces)]
+            cols = [slice(j * PIECE, (j + 1) * PIECE) for j in range(pieces)]
+            for j in range(pieces):
+                nc.vector.tensor_tensor(product[:, cols[j]], gains[:].indirect(lists[j]), x0_f[:, cols[j]], MULT)
+            for j in range(pieces):
+                nc.vector.tensor_tensor(x_f[:, cols[j]], shifts[:].indirect(lists[j]), product[:, cols[j]], ADD)
+                nc.scalar.copy(x_b[:, cols[j]], x_f[:, cols[j]])
+                for k in range(m_blocks):
+                    nc.tensor.matmul(
+                        banks[j, k][:],
+                        w_sb[:, b, k * P : (k + 1) * P],
+                        x_b[:, cols[j]],
+                        start=(b == 0),
+                        stop=(b == blocks - 1),
+                    )
+
+        for j in range(pieces):
+            for k in range(m_blocks):
+                staged = held.tile([P, PIECE], F32, name=f"staged{j}_{k}")
+                if k % 2 == 0:
+                    nc.scalar.copy(staged[:], banks[j, k][:])
+                else:
+                    nc.vector.tensor_copy(staged[:], banks[j, k][:])
+                nc.sync.dma_start(out[k * P : (k + 1) * P, j * PIECE : (j + 1) * PIECE], staged[:])

@@ -15,6 +15,7 @@ def tile_lookup_film_mul_none_kernel(tc, tab, x0, w, offs, out):
     ids = tab.shape[2]
     m = w.shape[1]
     blocks, pieces, m_blocks = rows // P, n // PIECE, m // P
+    halves = [slice(0, ids // 2), slice(ids // 2, ids)]
 
     with (
         tc.tile_pool(name="held", bufs=1) as held,
@@ -29,8 +30,12 @@ def tile_lookup_film_mul_none_kernel(tc, tab, x0, w, offs, out):
             x0_in.append(held.tile([P, n], BF16, name=f"x0_in{b}"))
             gains_in.append(held.tile([P, ids], BF16, name=f"gains_in{b}"))
             shifts_in.append(held.tile([P, ids], BF16, name=f"shifts_in{b}"))
+            if b == 0:
+                for h in halves:
+                    nc.sync.dma_start(gains_in[b][:, h], tab[0, r, h])
+            else:
+                nc.sync.dma_start(gains_in[b][:], tab[0, r, :])
             nc.sync.dma_start(x0_in[b][:], x0[r, :])
-            nc.sync.dma_start(gains_in[b][:], tab[0, r, :])
             nc.sync.dma_start(shifts_in[b][:], tab[1, r, :])
             if b == 0:
                 w_sb = held.tile([P, blocks, m], BF16, name="w_sb")
@@ -41,24 +46,38 @@ def tile_lookup_film_mul_none_kernel(tc, tab, x0, w, offs, out):
             for k in range(m_blocks):
                 banks[j, k] = psum.tile([P, PIECE], F32, name=f"bank{j}_{k}")
 
-        for b in range(blocks):
-            x0_f = held.tile([P, n], F32, name=f"x0_f{b}")
-            gains = held.tile([P, ids], F32, name=f"gains{b}")
-            shifts = held.tile([P, ids], F32, name=f"shifts{b}")
-            nc.vector.tensor_copy(x0_f[:], x0_in[b][:])
-            nc.scalar.copy(gains[:], gains_in[b][:])
-            nc.scalar.copy(shifts[:], shifts_in[b][:])
+        gains, shifts = [], []
 
+        def cast_tables(b):
+            gains.append(held.tile([P, ids], F32, name=f"gains{b}"))
+            shifts.append(held.tile([P, ids], F32, name=f"shifts{b}"))
+            if b == 0:
+                nc.vector.tensor_copy(gains[b][:, halves[0]], gains_in[b][:, halves[0]])
+                nc.scalar.copy(gains[b][:, halves[1]], gains_in[b][:, halves[1]])
+            else:
+                nc.scalar.copy(gains[b][:], gains_in[b][:])
+            nc.scalar.copy(shifts[b][:], shifts_in[b][:])
+
+        cast_tables(0)
+        for b in range(blocks):
+            if b + 1 < blocks:
+                cast_tables(b + 1)
+
+            x0_f = held.tile([P, n], F32, name=f"x0_f{b}")
+            nc.vector.tensor_copy(x0_f[:], x0_in[b][:])
             product = held.tile([P, n], F32, name=f"product{b}")
             x_f = held.tile([P, n], F32, name=f"x_f{b}")
             x_b = held.tile([P, n], BF16, name=f"x_b{b}")
             lists = [offsets[:, j * (PIECE // 16) : (j + 1) * (PIECE // 16)] for j in range(pieces)]
             cols = [slice(j * PIECE, (j + 1) * PIECE) for j in range(pieces)]
             for j in range(pieces):
-                nc.vector.tensor_tensor(product[:, cols[j]], gains[:].indirect(lists[j]), x0_f[:, cols[j]], MULT)
+                nc.vector.tensor_tensor(product[:, cols[j]], gains[b][:].indirect(lists[j]), x0_f[:, cols[j]], MULT)
             for j in range(pieces):
-                nc.vector.tensor_tensor(x_f[:, cols[j]], shifts[:].indirect(lists[j]), product[:, cols[j]], ADD)
-                nc.scalar.copy(x_b[:, cols[j]], x_f[:, cols[j]])
+                nc.vector.tensor_tensor(x_f[:, cols[j]], shifts[b][:].indirect(lists[j]), product[:, cols[j]], ADD)
+                if b == blocks - 1 and j == pieces - 1:
+                    nc.vector.tensor_copy(x_b[:, cols[j]], x_f[:, cols[j]])
+                else:
+                    nc.scalar.copy(x_b[:, cols[j]], x_f[:, cols[j]])
                 for k in range(m_blocks):
                     nc.tensor.matmul(
                         banks[j, k][:],

@@ -4,7 +4,9 @@ F32, BF16, U16 = mybir.dt.float32, mybir.dt.bfloat16, mybir.dt.uint16
 MULT, ADD = mybir.AluOpType.mult, mybir.AluOpType.add
 
 P = 128
-PIECE = 512
+
+PIECES = [slice(0, 512), slice(512, 768), slice(768, 1024)]
+GAIN_PIECES = [slice(0, 512), slice(512, 1024)]
 
 FLOPS = 2 * 512 * 1024 + 2 * 512 * 1024 * 256
 
@@ -14,8 +16,8 @@ def tile_lookup_film_mul_none_kernel(tc, tab, x0, w, offs, out):
     rows, n = x0.shape
     ids = tab.shape[2]
     m = w.shape[1]
-    blocks, pieces, m_blocks = rows // P, n // PIECE, m // P
-    halves = [slice(0, ids // 2), slice(ids // 2, ids)]
+    blocks, m_blocks = rows // P, m // P
+    quarters = [slice(q * ids // 4, (q + 1) * ids // 4) for q in range(4)]
 
     with (
         tc.tile_pool(name="held", bufs=1) as held,
@@ -31,67 +33,78 @@ def tile_lookup_film_mul_none_kernel(tc, tab, x0, w, offs, out):
             gains_in.append(held.tile([P, ids], BF16, name=f"gains_in{b}"))
             shifts_in.append(held.tile([P, ids], BF16, name=f"shifts_in{b}"))
             if b == 0:
-                for h in halves:
-                    nc.sync.dma_start(gains_in[b][:, h], tab[0, r, h])
+                nc.sync.dma_start(x0_in[b][:, GAIN_PIECES[0]], x0[r, GAIN_PIECES[0]])
+                for cols in quarters:
+                    nc.sync.dma_start(gains_in[b][:, cols], tab[0, r, cols])
+                nc.sync.dma_start(x0_in[b][:, GAIN_PIECES[1]], x0[r, GAIN_PIECES[1]])
             else:
+                nc.sync.dma_start(x0_in[b][:], x0[r, :])
                 nc.sync.dma_start(gains_in[b][:], tab[0, r, :])
-            nc.sync.dma_start(x0_in[b][:], x0[r, :])
             nc.sync.dma_start(shifts_in[b][:], tab[1, r, :])
             if b == 0:
                 w_sb = held.tile([P, blocks, m], BF16, name="w_sb")
                 nc.sync.dma_start(w_sb[:], w.rearrange("(b p) m -> p b m", p=P))
 
         banks = {}
-        for j in range(pieces):
+        for j, cols in enumerate(PIECES):
             for k in range(m_blocks):
-                banks[j, k] = psum.tile([P, PIECE], F32, name=f"bank{j}_{k}")
+                banks[j, k] = psum.tile([P, cols.stop - cols.start], F32, name=f"bank{j}_{k}")
 
-        gains, shifts = [], []
+        x0_f, gains, shifts = [], [], []
+
+        def cast_x0(b):
+            x0_f.append(held.tile([P, n], F32, name=f"x0_f{b}"))
+            for cols in GAIN_PIECES if b == 0 else [slice(0, n)]:
+                nc.vector.tensor_copy(x0_f[b][:, cols], x0_in[b][:, cols])
 
         def cast_tables(b):
             gains.append(held.tile([P, ids], F32, name=f"gains{b}"))
             shifts.append(held.tile([P, ids], F32, name=f"shifts{b}"))
             if b == 0:
-                nc.vector.tensor_copy(gains[b][:, halves[0]], gains_in[b][:, halves[0]])
-                nc.scalar.copy(gains[b][:, halves[1]], gains_in[b][:, halves[1]])
+                for q, cols in enumerate(quarters):
+                    if q % 2 == 0:
+                        nc.scalar.copy(gains[b][:, cols], gains_in[b][:, cols])
+                    else:
+                        nc.vector.tensor_copy(gains[b][:, cols], gains_in[b][:, cols])
             else:
                 nc.scalar.copy(gains[b][:], gains_in[b][:])
             nc.scalar.copy(shifts[b][:], shifts_in[b][:])
 
+        cast_x0(0)
         cast_tables(0)
         for b in range(blocks):
             if b + 1 < blocks:
                 cast_tables(b + 1)
 
-            x0_f = held.tile([P, n], F32, name=f"x0_f{b}")
-            nc.vector.tensor_copy(x0_f[:], x0_in[b][:])
+            if b > 0:
+                cast_x0(b)
             product = held.tile([P, n], F32, name=f"product{b}")
             x_f = held.tile([P, n], F32, name=f"x_f{b}")
             x_b = held.tile([P, n], BF16, name=f"x_b{b}")
-            lists = [offsets[:, j * (PIECE // 16) : (j + 1) * (PIECE // 16)] for j in range(pieces)]
-            cols = [slice(j * PIECE, (j + 1) * PIECE) for j in range(pieces)]
-            for j in range(pieces):
-                nc.vector.tensor_tensor(product[:, cols[j]], gains[b][:].indirect(lists[j]), x0_f[:, cols[j]], MULT)
-            for j in range(pieces):
-                nc.vector.tensor_tensor(x_f[:, cols[j]], shifts[b][:].indirect(lists[j]), product[:, cols[j]], ADD)
-                if b == blocks - 1 and j == pieces - 1:
-                    nc.vector.tensor_copy(x_b[:, cols[j]], x_f[:, cols[j]])
+            for cols in GAIN_PIECES:
+                piece = offsets[:, cols.start // 16 : cols.stop // 16]
+                nc.vector.tensor_tensor(product[:, cols], gains[b][:].indirect(piece), x0_f[b][:, cols], MULT)
+            for j, cols in enumerate(PIECES):
+                piece = offsets[:, cols.start // 16 : cols.stop // 16]
+                nc.vector.tensor_tensor(x_f[:, cols], shifts[b][:].indirect(piece), product[:, cols], ADD)
+                if b == blocks - 1 and j == len(PIECES) - 1:
+                    nc.vector.tensor_copy(x_b[:, cols], x_f[:, cols])
                 else:
-                    nc.scalar.copy(x_b[:, cols[j]], x_f[:, cols[j]])
+                    nc.scalar.copy(x_b[:, cols], x_f[:, cols])
                 for k in range(m_blocks):
                     nc.tensor.matmul(
                         banks[j, k][:],
                         w_sb[:, b, k * P : (k + 1) * P],
-                        x_b[:, cols[j]],
+                        x_b[:, cols],
                         start=(b == 0),
                         stop=(b == blocks - 1),
                     )
 
-        for j in range(pieces):
+        for j, cols in enumerate(PIECES):
             for k in range(m_blocks):
-                staged = held.tile([P, PIECE], F32, name=f"staged{j}_{k}")
+                staged = held.tile([P, cols.stop - cols.start], F32, name=f"staged{j}_{k}")
                 if k % 2 == 0:
                     nc.scalar.copy(staged[:], banks[j, k][:])
                 else:
                     nc.vector.tensor_copy(staged[:], banks[j, k][:])
-                nc.sync.dma_start(out[k * P : (k + 1) * P, j * PIECE : (j + 1) * PIECE], staged[:])
+                nc.sync.dma_start(out[k * P : (k + 1) * P, cols], staged[:])

import concourse.mybir as mybir

F32, BF16, U16 = mybir.dt.float32, mybir.dt.bfloat16, mybir.dt.uint16
MULT, ADD = mybir.AluOpType.mult, mybir.AluOpType.add

P = 128

PIECES = [slice(0, 512), slice(512, 768), slice(768, 1024)]
GAIN_PIECES = [slice(0, 512), slice(512, 1024)]

FLOPS = 2 * 512 * 1024 + 2 * 512 * 1024 * 256


def tile_lookup_film_mul_none_kernel(tc, tab, x0, w, offs, out):
    nc = tc.nc
    rows, n = x0.shape
    ids = tab.shape[2]
    m = w.shape[1]
    blocks, m_blocks = rows // P, m // P
    quarters = [slice(q * ids // 4, (q + 1) * ids // 4) for q in range(4)]

    with (
        tc.tile_pool(name="held", bufs=1) as held,
        tc.psum_pool(name="psum", bufs=1) as psum,
    ):
        offsets = held.tile([P, n // 16], U16, name="offsets")
        nc.sync.dma_start(offsets[:], offs)

        x0_in, gains_in, shifts_in = [], [], []
        for b in range(blocks):
            r = slice(b * P, (b + 1) * P)
            x0_in.append(held.tile([P, n], BF16, name=f"x0_in{b}"))
            gains_in.append(held.tile([P, ids], BF16, name=f"gains_in{b}"))
            shifts_in.append(held.tile([P, ids], BF16, name=f"shifts_in{b}"))
            if b == 0:
                nc.sync.dma_start(x0_in[b][:, GAIN_PIECES[0]], x0[r, GAIN_PIECES[0]])
                for cols in quarters:
                    nc.sync.dma_start(gains_in[b][:, cols], tab[0, r, cols])
                nc.sync.dma_start(x0_in[b][:, GAIN_PIECES[1]], x0[r, GAIN_PIECES[1]])
            else:
                nc.sync.dma_start(x0_in[b][:], x0[r, :])
                nc.sync.dma_start(gains_in[b][:], tab[0, r, :])
            nc.sync.dma_start(shifts_in[b][:], tab[1, r, :])
            if b == 0:
                w_sb = held.tile([P, blocks, m], BF16, name="w_sb")
                nc.sync.dma_start(w_sb[:], w.rearrange("(b p) m -> p b m", p=P))

        banks = {}
        for j, cols in enumerate(PIECES):
            for k in range(m_blocks):
                banks[j, k] = psum.tile([P, cols.stop - cols.start], F32, name=f"bank{j}_{k}")

        x0_f, gains, shifts = [], [], []

        def cast_x0(b):
            x0_f.append(held.tile([P, n], F32, name=f"x0_f{b}"))
            for cols in GAIN_PIECES if b == 0 else [slice(0, n)]:
                nc.vector.tensor_copy(x0_f[b][:, cols], x0_in[b][:, cols])

        def cast_tables(b):
            gains.append(held.tile([P, ids], F32, name=f"gains{b}"))
            shifts.append(held.tile([P, ids], F32, name=f"shifts{b}"))
            if b == 0:
                for q, cols in enumerate(quarters):
                    if q % 2 == 0:
                        nc.scalar.copy(gains[b][:, cols], gains_in[b][:, cols])
                    else:
                        nc.vector.tensor_copy(gains[b][:, cols], gains_in[b][:, cols])
            else:
                nc.scalar.copy(gains[b][:], gains_in[b][:])
            nc.scalar.copy(shifts[b][:], shifts_in[b][:])

        cast_x0(0)
        cast_tables(0)
        for b in range(blocks):
            if b + 1 < blocks:
                cast_tables(b + 1)

            if b > 0:
                cast_x0(b)
            product = held.tile([P, n], F32, name=f"product{b}")
            x_f = held.tile([P, n], F32, name=f"x_f{b}")
            x_b = held.tile([P, n], BF16, name=f"x_b{b}")
            for cols in GAIN_PIECES:
                piece = offsets[:, cols.start // 16 : cols.stop // 16]
                nc.vector.tensor_tensor(product[:, cols], gains[b][:].indirect(piece), x0_f[b][:, cols], MULT)
            for j, cols in enumerate(PIECES):
                piece = offsets[:, cols.start // 16 : cols.stop // 16]
                nc.vector.tensor_tensor(x_f[:, cols], shifts[b][:].indirect(piece), product[:, cols], ADD)
                if b == blocks - 1 and j == len(PIECES) - 1:
                    nc.vector.tensor_copy(x_b[:, cols], x_f[:, cols])
                else:
                    nc.scalar.copy(x_b[:, cols], x_f[:, cols])
                for k in range(m_blocks):
                    nc.tensor.matmul(
                        banks[j, k][:],
                        w_sb[:, b, k * P : (k + 1) * P],
                        x_b[:, cols],
                        start=(b == 0),
                        stop=(b == blocks - 1),
                    )

        for j, cols in enumerate(PIECES):
            for k in range(m_blocks):
                staged = held.tile([P, cols.stop - cols.start], F32, name=f"staged{j}_{k}")
                if k % 2 == 0:
                    nc.scalar.copy(staged[:], banks[j, k][:])
                else:
                    nc.vector.tensor_copy(staged[:], banks[j, k][:])
                nc.sync.dma_start(out[k * P : (k + 1) * P, cols], staged[:])
